import numpy as np
import ml_dtypes


def mxq(x, axis, fmt="e4m3"):
    dtype, down = {"e4m3": (ml_dtypes.float8_e4m3fn, 7), "e5m2": (ml_dtypes.float8_e5m2, 14)}[fmt]
    v = np.moveaxis(np.asarray(x, np.float32).astype(ml_dtypes.bfloat16).astype(np.float64), axis, -1)
    blocks = v.reshape(v.shape[:-1] + (-1, 32))
    amax = np.abs(blocks).max(-1, keepdims=True)
    byte = np.maximum(np.where(amax > 0, np.frexp(amax)[1] - 1 + 127, 0) - down, 1)
    scale = np.exp2(byte - 127.0)
    codes = (blocks / scale).astype(np.float32).astype(dtype).astype(np.float64)
    return np.moveaxis((codes * scale).reshape(v.shape), -1, axis)


WIDE = False


def mx_kscale(k):
    if not WIDE:
        return np.ones(k)
    levels = np.array([10, -10, 5, -5, 0])
    if k % 512:
        return np.exp2(np.random.permutation(np.resize(levels, k // 32))).repeat(32)
    a = np.empty((k // 512, 16))
    for p in range(k // 512):
        a[p, :8] = np.random.permutation(np.resize(levels, 8))
        for g in range(8):
            far = levels[np.abs(levels - a[p, g]) >= 10]
            a[p, g + 8] = far[np.random.randint(len(far))]
    return np.exp2(a.ravel()).repeat(32)


def f64(x):
    return np.asarray(x).astype(np.float64)


def striped(idx):
    return np.tile(idx.reshape(-1, 16).T, (8, 1)).astype(np.uint16)


def unstriped(offs):
    return offs[:16].T.reshape(-1).astype(np.int64)


E2M1 = np.array([0.0, 0.5, 1.0, 1.5, 2.0, 3.0, 4.0, 6.0, -0.0, -0.5, -1.0, -1.5, -2.0, -3.0, -4.0, -6.0])


def pack_fp4(w):
    k, n = w.shape
    w = f64(np.asarray(w, np.float32).astype(ml_dtypes.bfloat16)).reshape(k // 32, 32, n)
    amax = np.abs(w).max(1)
    mant, ex = np.frexp(amax / 6.0)
    byte = np.clip(np.where(amax > 0, np.where(mant > 0.5, ex, ex - 1) + 127, 1), 1, 254)
    scaled = (w * np.exp2(127.0 - byte)[:, None, :]).reshape(k, n).astype(np.float32)
    c = np.ascontiguousarray(scaled.reshape(k // 512, 128, 4, n).transpose(0, 1, 3, 2)).astype(ml_dtypes.float4_e2m1fn).view(np.uint8) & 0xF
    words = (c[..., 0::2] | (c[..., 1::2] << 4)).reshape(k // 512, 128, 2 * n)
    return np.ascontiguousarray(words), np.ascontiguousarray(byte.astype(np.uint8).reshape(k // 512, 16, n))


def unpack_fp4(words, scales):
    g, _, n = scales.shape
    words = np.ascontiguousarray(words).reshape(g, 128, n, 2)
    nib = np.empty((g, 128, n, 4), np.uint8)
    nib[..., 0::2] = words & 0xF
    nib[..., 1::2] = words >> 4
    vals = E2M1[nib] * np.repeat(np.exp2(scales.astype(np.float64) - 127.0), 8, axis=1)[..., None]
    return vals.transpose(0, 1, 3, 2).reshape(g * 512, n)


def sigmoid(v):
    return 1.0 / (1.0 + np.exp(-np.maximum(v, -700.0)))


K, T, N = 512, 512, 256


def setup_inputs():
    n = np.random.standard_normal
    s = mx_kscale(K)[:, None]
    packed_xT = pack_fp4(n((K, T)) * s)
    return {
        "x_words": packed_xT[0],
        "x_scales": packed_xT[1],
        "w1": (n((K, N)) / np.sqrt(K) / s).astype(np.float32),
        "w2": (n((K, N)) / np.sqrt(K) / s).astype(np.float32),
        "w3": (n((K, N)) / np.sqrt(K) / s).astype(np.float32),
        "pos1": striped(np.random.permutation(T)),
        "pos2": striped(np.random.permutation(T)),
        "pos3": striped(np.random.permutation(T)),
    }


def reference(x_words, x_scales, w1, w2, w3, pos1, pos2, pos3):
    xq = unpack_fp4(x_words, x_scales)
    y = mxq(f64(w1), 0, "e4m3").T @ xq
    e = mxq(f64(w2), 0, "e4m3").T @ xq
    h = mxq(f64(w3), 0, "e4m3").T @ xq
    z = (sigmoid(y + e[:, unstriped(pos1)])) * h[:, unstriped(pos1)] + (sigmoid(y + e[:, unstriped(pos2)])) * h[:, unstriped(pos2)] + (sigmoid(y + e[:, unstriped(pos3)])) * h[:, unstriped(pos3)]
    return z

@@ -1,0 +1,150 @@
+from contextlib import ExitStack
+
+import concourse.mybir as mybir
+
+K, T, N = 512, 512, 256
+FLOPS = 3 * 2 * K * T * N
+
+F32 = mybir.dt.float32
+BF16 = mybir.dt.bfloat16
+I32 = mybir.dt.int32
+U32 = mybir.dt.uint32
+U16 = mybir.dt.uint16
+U8 = mybir.dt.uint8
+FP8X4 = mybir.dt.float8_e4m3fn_x4
+FP4X4 = mybir.dt.float4_e2m1fn_x4
+MULT = mybir.AluOpType.mult
+ADD = mybir.AluOpType.add
+SIGMOID = mybir.ActivationFunctionType.Sigmoid
+
+P = 128
+PACK = 4
+E_WIDTH = 704
+H_WIDTH = 528
+
+
+def tile_picked_wgatedg_none_l_kernel(tc, x_words, x_scales, w1, w2, w3, pos1, pos2, pos3, out):
+    nc = tc.nc
+    with ExitStack() as ctx:
+        keep = ctx.enter_context(tc.tile_pool(name="keep", bufs=1))
+        psum = ctx.enter_context(tc.psum_pool(name="psum", bufs=1))
+
+        def sb(name, shape, dtype, tag=None):
+            return keep.tile(shape, dtype, name=name, tag=tag or name, align_bytes=64)
+
+        xw = sb("xw", [P, 2 * T], U8)
+        xs = sb("xs", [P, T], U8)
+        lists = [sb("pos%d" % d, [P, T // 16], U16) for d in range(3)]
+        raw2 = [sb("raw2_%d" % b, [P, PACK, P], F32) for b in range(2)]
+        raw1 = [sb("raw1_%d" % b, [P, PACK, P], F32) for b in range(2)]
+        raw3 = sb("raw3", [P, PACK, N], F32)
+        e_t = [sb("e%d" % b, [P, E_WIDTH], F32) for b in range(2)]
+        h_t = [sb("h%d" % b, [P, H_WIDTH], F32) for b in range(2)]
+        y_t = [sb("y%d" % b, [P, T], F32) for b in range(2)]
+        warm = sb("warm", [P, 2], F32)
+
+        nc.vector.memset(xs[:].bitcast(I32), 0)
+        nc.vector.memset(warm[:, 0:1], 0.0)
+
+        def rows(w):
+            return w.rearrange("(p j) n -> p j n", j=PACK)
+
+        nc.sync.dma_start(raw2[0][:], rows(w2)[:, :, 0:P])
+        nc.sync.dma_start(xw[:].bitcast(I32), x_words[0].bitcast(I32))
+        for q in range(4):
+            nc.sync.dma_start(xs[32 * q : 32 * q + 4, :].bitcast(I32), x_scales[0, 4 * q : 4 * q + 4, :].bitcast(I32))
+        nc.scalar.activation(warm[:, 1:2], warm[:, 0:1], SIGMOID)
+        nc.sync.dma_start(lists[0][:], pos1)
+        nc.sync.dma_start(raw1[0][:], rows(w1)[:, :, 0:P])
+        nc.sync.dma_start(raw2[1][:], rows(w2)[:, :, P:N])
+        nc.sync.dma_start(lists[1][:], pos2)
+        nc.sync.dma_start(raw1[1][:], rows(w1)[:, :, P:N])
+        nc.sync.dma_start(lists[2][:], pos3)
+        nc.sync.dma_start(raw3[:], rows(w3))
+
+        for b in range(2):
+            nc.gpsimd.memset(e_t[b][:, T:E_WIDTH], 0.0)
+        for b in range(2):
+            nc.gpsimd.memset(h_t[b][:, T:H_WIDTH], 0.0)
+
+        def quantise(name, raw, cast, tag=None):
+            grouped = sb(name + "_bf", [P, P, PACK], BF16, tag)
+            codes = sb(name + "_codes", [P, P], U32)
+            scales = sb(name + "_scales", [P, P], U8)
+            cast(grouped[:], raw.rearrange("p j w -> p w j"))
+            nc.vector.quantize_mx(codes[:].bitcast(FP8X4), scales[:], grouped[:].rearrange("p w j -> p (w j)"))
+            return codes, scales
+
+        def product(wq, c0, c1, tag):
+            bank = psum.tile([P, T], F32, name=tag)
+            codes, scales = wq
+            nc.tensor.matmul_mx(
+                bank[:, 0 : c1 - c0],
+                lhsT=codes[:].bitcast(FP8X4),
+                lhsT_scale=scales[:],
+                rhs=xw[:, 2 * c0 : 2 * c1].bitcast(FP4X4),
+                rhs_scale=xs[:, c0:c1],
+                start=True,
+                stop=True,
+            )
+            return bank
+
+        q20 = quantise("w20", raw2[0][:], nc.vector.tensor_copy)
+        lo = product(q20, 0, T // 2, "mm0")
+        hi = product(q20, T // 2, T, "mm1")
+        nc.vector.tensor_copy(e_t[0][:, 0 : T // 2], lo[:, 0 : T // 2])
+        nc.vector.tensor_copy(e_t[0][:, T // 2 : T], hi[:, 0 : T // 2])
+
+        q10 = quantise("w10", raw1[0][:], nc.scalar.copy)
+        q21 = quantise("w21", raw2[1][:], nc.scalar.copy)
+        nc.scalar.copy(y_t[0][:], product(q10, 0, T, "mm2")[:])
+        nc.scalar.copy(e_t[1][:, 0:T], product(q21, 0, T, "mm0")[:])
+
+        after = {0: "w10_bf", 1: "w21_bf", 3: "w11_bf", 5: "w31_bf", 6: "e1"}
+        gates = {}
+        picks = {}
+        terms = {}
+        pres = {}
+
+        def front(u):
+            b, d = divmod(u, 3)
+            picked = sb("eg%d" % u, [P, T], F32, after.get(u))
+            picks[u] = picked
+            nc.vector.tensor_copy(picked[:], e_t[b][:].indirect(lists[d][:]))
+
+        def rear(u, add, y):
+            pre = keep.tile([P, T], F32, name="pre%d" % u)
+            add(pre[:], picks[u][:], y[:], ADD)
+            gate = keep.tile([P, T], F32, name="gate%d" % u)
+            nc.scalar.activation(gate[:], pre[:], SIGMOID)
+            gates[u] = gate
+
+        q11 = quantise("w11", raw1[1][:], nc.scalar.copy)
+        q30 = quantise("w30", raw3[:, :, 0:P], nc.scalar.copy)
+        y1_bank = product(q11, 0, T, "mm3")
+        nc.scalar.copy(y_t[1][:], y1_bank[:])
+        nc.scalar.copy(h_t[0][:, 0:T], product(q30, 0, T, "mm1")[:])
+        q31 = quantise("w31", raw3[:, :, P:N], nc.scalar.copy)
+        for u in range(5):
+            front(u)
+            rear(u, nc.gpsimd.tensor_tensor, y_t[u // 3])
+        nc.scalar.copy(h_t[1][:, 0:T], product(q31, 0, T, "mm4")[:])
+        front(5)
+
+        for b in range(2):
+            for d in range(3):
+                terms[3 * b + d] = sb("term%d_%d" % (b, d), [P, T], F32, after.get(6 + 3 * b + d))
+            pair = keep.tile([P, T], F32, name="pair%d" % b)
+            total = keep.tile([P, T], F32, name="total%d" % b)
+            for d in range(2):
+                nc.vector.tensor_tensor(terms[3 * b + d][:], h_t[b][:].indirect(lists[d][:]), gates[3 * b + d][:], MULT)
+                if b == 0 and d == 0:
+                    rear(5, nc.vector.tensor_tensor, y1_bank)
+            halves = [(0, T)] if b == 0 else [(0, T // 2), (T // 2, T)]
+            for i, (c0, c1) in enumerate(halves):
+                nc.vector.tensor_tensor(terms[3 * b + 2][:, c0:c1], h_t[b][:].indirect(lists[2][:, c0 // 16 : c1 // 16]), gates[3 * b + 2][:, c0:c1], MULT)
+                if i == 0:
+                    nc.vector.tensor_tensor(pair[:], terms[3 * b][:], terms[3 * b + 1][:], ADD)
+            for c0, c1 in halves:
+                nc.vector.tensor_tensor(total[:, c0:c1], pair[:, c0:c1], terms[3 * b + 2][:, c0:c1], ADD)
+                nc.sync.dma_start(out[P * b : P * (b + 1), c0:c1], total[:, c0:c1])

@@ -1,6 +1,7 @@
 from contextlib import ExitStack
 
 import concourse.mybir as mybir
+from concourse.masks import make_identity
 
 K, T, N = 512, 512, 256
 FLOPS = 3 * 2 * K * T * N
@@ -19,8 +20,14 @@ SIGMOID = mybir.ActivationFunctionType.Sigmoid
 
 P = 128
 PACK = 4
-E_WIDTH = 704
-H_WIDTH = 528
+WINDOW = 704
+
+AFTER = {"E3": "w10_bf", "E2": "w10_bf", "H4": "w11_bf", "H2": "eg1", "H3": "w30_bf", "H1": "eg0"}
+ADDER = ["G", "P", "G", "G", "G", "P"]
+MULER = ["G", "G", "G", "C", "V", "V"]
+SUMMER = ["V", "V", "V", "V"]
+PREP = ["y0", "h0", "e1", "h1", "y1"]
+ORDER = ["E2", "E1", "E5", "H2", "E4", "E3", "E0", "H0", "H5", "H4", "H1", "H3"]
 
 
 def tile_picked_wgatedg_none_l_kernel(tc, x_words, x_scales, w1, w2, w3, pos1, pos2, pos3, out):
@@ -38,13 +45,20 @@ def tile_picked_wgatedg_none_l_kernel(tc, x_words, x_scales, w1, w2, w3, pos1, p
         raw2 = [sb("raw2_%d" % b, [P, PACK, P], F32) for b in range(2)]
         raw1 = [sb("raw1_%d" % b, [P, PACK, P], F32) for b in range(2)]
         raw3 = sb("raw3", [P, PACK, N], F32)
-        e_t = [sb("e%d" % b, [P, E_WIDTH], F32) for b in range(2)]
-        h_t = [sb("h%d" % b, [P, H_WIDTH], F32) for b in range(2)]
+        e_t = [sb("e%d" % b, [P, WINDOW], F32) for b in range(2)]
+        h_t = [sb("h%d" % b, [P, WINDOW], F32) for b in range(2)]
         y_t = [sb("y%d" % b, [P, T], F32) for b in range(2)]
         warm = sb("warm", [P, 2], F32)
+        ident = sb("ident", [P, P], F32)
 
         nc.vector.memset(xs[:].bitcast(I32), 0)
         nc.vector.memset(warm[:, 0:1], 0.0)
+        nc.scalar.activation(warm[:, 1:2], warm[:, 0:1], SIGMOID)
+        make_identity(nc, ident[:])
+        for b in range(2):
+            nc.gpsimd.memset(e_t[b][:, T:WINDOW], 0.0)
+        for b in range(2):
+            nc.gpsimd.memset(h_t[b][:, T:WINDOW], 0.0)
 
         def rows(w):
             return w.rearrange("(p j) n -> p j n", j=PACK)
@@ -53,30 +67,24 @@ def tile_picked_wgatedg_none_l_kernel(tc, x_words, x_scales, w1, w2, w3, pos1, p
         nc.sync.dma_start(xw[:].bitcast(I32), x_words[0].bitcast(I32))
         for q in range(4):
             nc.sync.dma_start(xs[32 * q : 32 * q + 4, :].bitcast(I32), x_scales[0, 4 * q : 4 * q + 4, :].bitcast(I32))
-        nc.scalar.activation(warm[:, 1:2], warm[:, 0:1], SIGMOID)
-        nc.sync.dma_start(lists[0][:], pos1)
         nc.sync.dma_start(raw1[0][:], rows(w1)[:, :, 0:P])
         nc.sync.dma_start(raw2[1][:], rows(w2)[:, :, P:N])
-        nc.sync.dma_start(lists[1][:], pos2)
         nc.sync.dma_start(raw1[1][:], rows(w1)[:, :, P:N])
-        nc.sync.dma_start(lists[2][:], pos3)
+        nc.sync.dma_start(lists[0][:], pos1)
         nc.sync.dma_start(raw3[:], rows(w3))
+        nc.sync.dma_start(lists[2][:], pos3)
+        nc.sync.dma_start(lists[1][:], pos2)
 
-        for b in range(2):
-            nc.gpsimd.memset(e_t[b][:, T:E_WIDTH], 0.0)
-        for b in range(2):
-            nc.gpsimd.memset(h_t[b][:, T:H_WIDTH], 0.0)
-
-        def quantise(name, raw, cast, tag=None):
-            grouped = sb(name + "_bf", [P, P, PACK], BF16, tag)
+        def quantise(name, raw, cast):
+            grouped = sb(name + "_bf", [P, P, PACK], BF16)
             codes = sb(name + "_codes", [P, P], U32)
             scales = sb(name + "_scales", [P, P], U8)
             cast(grouped[:], raw.rearrange("p j w -> p w j"))
             nc.vector.quantize_mx(codes[:].bitcast(FP8X4), scales[:], grouped[:].rearrange("p w j -> p (w j)"))
             return codes, scales
 
-        def product(wq, c0, c1, tag):
-            bank = psum.tile([P, T], F32, name=tag)
+        def product(wq, c0, c1, name, tag):
+            bank = psum.tile([P, T], F32, name=name, tag=tag)
             codes, scales = wq
             nc.tensor.matmul_mx(
                 bank[:, 0 : c1 - c0],
@@ -90,61 +98,80 @@ def tile_picked_wgatedg_none_l_kernel(tc, x_words, x_scales, w1, w2, w3, pos1, p
             return bank
 
         q20 = quantise("w20", raw2[0][:], nc.vector.tensor_copy)
-        lo = product(q20, 0, T // 2, "mm0")
-        hi = product(q20, T // 2, T, "mm1")
+        lo = product(q20, 0, T // 2, "e0a", "A")
+        hi = product(q20, T // 2, T, "e0b", "B")
         nc.vector.tensor_copy(e_t[0][:, 0 : T // 2], lo[:, 0 : T // 2])
         nc.vector.tensor_copy(e_t[0][:, T // 2 : T], hi[:, 0 : T // 2])
 
-        q10 = quantise("w10", raw1[0][:], nc.scalar.copy)
-        q21 = quantise("w21", raw2[1][:], nc.scalar.copy)
-        nc.scalar.copy(y_t[0][:], product(q10, 0, T, "mm2")[:])
-        nc.scalar.copy(e_t[1][:, 0:T], product(q21, 0, T, "mm0")[:])
+        y_bank = {}
+        for step in PREP:
+            b = int(step[1])
+            if step[0] == "y":
+                y_bank[b] = product(quantise("w1%d" % b, raw1[b][:], nc.scalar.copy), 0, T, step, "Y%d" % b)
+                if any(ADDER[3 * b + d] != "V" for d in range(3)):
+                    nc.scalar.copy(y_t[b][:], y_bank[b][:])
+            elif step[0] == "e":
+                nc.scalar.copy(e_t[1][:, 0:T], product(quantise("w21", raw2[1][:], nc.scalar.copy), 0, T, step, "A")[:])
+            else:
+                wq = quantise("w3%d" % b, raw3[:, :, P * b : P * (b + 1)], nc.scalar.copy)
+                nc.scalar.copy(h_t[b][:, 0:T], product(wq, 0, T, step, "B")[:])
 
-        after = {0: "w10_bf", 1: "w21_bf", 3: "w11_bf", 5: "w31_bf", 6: "e1"}
+        engine = {"G": nc.gpsimd, "V": nc.vector}
         gates = {}
-        picks = {}
         terms = {}
-        pres = {}
+        pairs = {}
+        made = [[], []]
+        turns = []
 
-        def front(u):
+        def gate_of(u):
             b, d = divmod(u, 3)
-            picked = sb("eg%d" % u, [P, T], F32, after.get(u))
-            picks[u] = picked
+            picked = sb("eg%d" % u, [P, T], F32, AFTER.get("E%d" % u))
             nc.vector.tensor_copy(picked[:], e_t[b][:].indirect(lists[d][:]))
+            pre = sb("pre%d" % u, [P, T], F32)
+            source = pre
+            if ADDER[u] == "G":
+                nc.gpsimd.tensor_tensor(pre[:], picked[:], y_t[b][:], ADD)
+            elif ADDER[u] == "V":
+                nc.vector.tensor_tensor(pre[:], picked[:], y_bank[b][:], ADD)
+            else:
+                k = len(turns) % 2
+                turns.append(u)
+                turned = psum.tile([P, T], F32, name="turned%d" % u, tag="turn%d" % k)
+                for i, src in enumerate((y_t[b], picked)):
+                    for j in range(4):
+                        cols = slice(P * j, P * (j + 1))
+                        nc.tensor.matmul(turned[:, cols], src[:, cols], ident[:], start=(i == 0 and j == 0), stop=(i == 1 and j == 3), is_transpose=True)
+                nc.scalar.copy(pre[:], turned[:])
+                source = psum.tile([P, T], F32, name="back%d" % u, tag="back%d" % k)
+                for j in range(4):
+                    cols = slice(P * j, P * (j + 1))
+                    nc.tensor.transpose(source[:, cols], pre[:, cols], ident[:])
+            gates[u] = sb("gate%d" % u, [P, T], F32)
+            nc.scalar.activation(gates[u][:], source[:], SIGMOID)
 
-        def rear(u, add, y):
-            pre = keep.tile([P, T], F32, name="pre%d" % u)
-            add(pre[:], picks[u][:], y[:], ADD)
-            gate = keep.tile([P, T], F32, name="gate%d" % u)
-            nc.scalar.activation(gate[:], pre[:], SIGMOID)
-            gates[u] = gate
+        def term_of(u, pieces):
+            b, d = divmod(u, 3)
+            picked = sb("hg%d" % u, [P, T], F32, AFTER.get("H%d" % u))
+            terms[u] = picked if MULER[u] == "C" else sb("term%d" % u, [P, T], F32)
+            for c0, c1 in pieces:
+                looked_up = h_t[b][:].indirect(lists[d][:, c0 // 16 : c1 // 16])
+                if MULER[u] == "C":
+                    nc.vector.tensor_tensor(picked[:, c0:c1], looked_up, gates[u][:, c0:c1], MULT)
+                else:
+                    nc.vector.tensor_copy(picked[:, c0:c1], looked_up)
+                    engine[MULER[u]].tensor_tensor(terms[u][:, c0:c1], picked[:, c0:c1], gates[u][:, c0:c1], MULT)
+            made[b].append(u)
+            if len(made[b]) == 2:
+                pairs[b] = sb("pair%d" % b, [P, T], F32)
+                engine[SUMMER[2 * b]].tensor_tensor(pairs[b][:], terms[made[b][0]][:], terms[made[b][1]][:], ADD)
+            if len(made[b]) == 3:
+                total = sb("total%d" % b, [P, T], F32)
+                for c0, c1 in pieces:
+                    engine[SUMMER[2 * b + 1]].tensor_tensor(total[:, c0:c1], pairs[b][:, c0:c1], terms[u][:, c0:c1], ADD)
+                    nc.sync.dma_start(out[P * b : P * (b + 1), c0:c1], total[:, c0:c1])
 
-        q11 = quantise("w11", raw1[1][:], nc.scalar.copy)
-        q30 = quantise("w30", raw3[:, :, 0:P], nc.scalar.copy)
-        y1_bank = product(q11, 0, T, "mm3")
-        nc.scalar.copy(y_t[1][:], y1_bank[:])
-        nc.scalar.copy(h_t[0][:, 0:T], product(q30, 0, T, "mm1")[:])
-        q31 = quantise("w31", raw3[:, :, P:N], nc.scalar.copy)
-        for u in range(5):
-            front(u)
-            rear(u, nc.gpsimd.tensor_tensor, y_t[u // 3])
-        nc.scalar.copy(h_t[1][:, 0:T], product(q31, 0, T, "mm4")[:])
-        front(5)
-
-        for b in range(2):
-            for d in range(3):
-                terms[3 * b + d] = sb("term%d_%d" % (b, d), [P, T], F32, after.get(6 + 3 * b + d))
-            pair = keep.tile([P, T], F32, name="pair%d" % b)
-            total = keep.tile([P, T], F32, name="total%d" % b)
-            for d in range(2):
-                nc.vector.tensor_tensor(terms[3 * b + d][:], h_t[b][:].indirect(lists[d][:]), gates[3 * b + d][:], MULT)
-                if b == 0 and d == 0:
-                    rear(5, nc.vector.tensor_tensor, y1_bank)
-            halves = [(0, T)] if b == 0 else [(0, T // 2), (T // 2, T)]
-            for i, (c0, c1) in enumerate(halves):
-                nc.vector.tensor_tensor(terms[3 * b + 2][:, c0:c1], h_t[b][:].indirect(lists[2][:, c0 // 16 : c1 // 16]), gates[3 * b + 2][:, c0:c1], MULT)
-                if i == 0:
-                    nc.vector.tensor_tensor(pair[:], terms[3 * b][:], terms[3 * b + 1][:], ADD)
-            for c0, c1 in halves:
-                nc.vector.tensor_tensor(total[:, c0:c1], pair[:, c0:c1], terms[3 * b + 2][:, c0:c1], ADD)
-                nc.sync.dma_start(out[P * b : P * (b + 1), c0:c1], total[:, c0:c1])
+        for step in ORDER:
+            if step[0] == "E":
+                gate_of(int(step[1]))
+            else:
+                term_of(int(step[1]), [(0, T // 2), (T // 2, T)] if step == ORDER[-1] else [(0, T)])

@@ -22,12 +22,12 @@ P = 128
 PACK = 4
 WINDOW = 704
 
-AFTER = {"E3": "w10_bf", "E2": "w10_bf", "H4": "w11_bf", "H2": "eg1", "H3": "w30_bf", "H1": "eg0"}
-ADDER = ["G", "P", "G", "G", "G", "P"]
-MULER = ["G", "G", "G", "C", "V", "V"]
-SUMMER = ["V", "V", "V", "V"]
-PREP = ["y0", "h0", "e1", "h1", "y1"]
-ORDER = ["E2", "E1", "E5", "H2", "E4", "E3", "E0", "H0", "H5", "H4", "H1", "H3"]
+AFTER = {"pre4": "w31bf", "pre3": "eg4", "gate3": "w10bf", "eg1": "eg5", "pre1": "w31bf", "gate1": "eg0", "pre2": "w20bf", "gate2": "eg5", "hg4": "e1", "hg2": "gate4", "hg3": "pre5", "hg0": "w21bf"}
+ADDER = ["G", "P", "G", "G", "P", "P"]
+MULER = ["C", "C", "C", "C", "C", "C"]
+SUMMER = ["V", "V", "P", "P"]
+CAST = {}
+ORDER = ["y0", "e1", "y1", "E5", "h1", "E4", "E0", "H5", "E3", "E1", "E2", "H4", "h0", "H2", "H3", "H0", "H1"]
 
 
 def tile_picked_wgatedg_none_l_kernel(tc, x_words, x_scales, w1, w2, w3, pos1, pos2, pos3, out):
@@ -36,8 +36,8 @@ def tile_picked_wgatedg_none_l_kernel(tc, x_words, x_scales, w1, w2, w3, pos1, p
         keep = ctx.enter_context(tc.tile_pool(name="keep", bufs=1))
         psum = ctx.enter_context(tc.psum_pool(name="psum", bufs=1))
 
-        def sb(name, shape, dtype, tag=None):
-            return keep.tile(shape, dtype, name=name, tag=tag or name, align_bytes=64)
+        def sb(name, shape, dtype):
+            return keep.tile(shape, dtype, name=name, tag=AFTER.get(name, name), align_bytes=64)
 
         xw = sb("xw", [P, 2 * T], U8)
         xs = sb("xs", [P, T], U8)
@@ -67,16 +67,16 @@ def tile_picked_wgatedg_none_l_kernel(tc, x_words, x_scales, w1, w2, w3, pos1, p
         nc.sync.dma_start(xw[:].bitcast(I32), x_words[0].bitcast(I32))
         for q in range(4):
             nc.sync.dma_start(xs[32 * q : 32 * q + 4, :].bitcast(I32), x_scales[0, 4 * q : 4 * q + 4, :].bitcast(I32))
-        nc.sync.dma_start(raw1[0][:], rows(w1)[:, :, 0:P])
         nc.sync.dma_start(raw2[1][:], rows(w2)[:, :, P:N])
         nc.sync.dma_start(raw1[1][:], rows(w1)[:, :, P:N])
-        nc.sync.dma_start(lists[0][:], pos1)
-        nc.sync.dma_start(raw3[:], rows(w3))
+        nc.sync.dma_start(raw1[0][:], rows(w1)[:, :, 0:P])
         nc.sync.dma_start(lists[2][:], pos3)
         nc.sync.dma_start(lists[1][:], pos2)
+        nc.sync.dma_start(raw3[:], rows(w3))
+        nc.sync.dma_start(lists[0][:], pos1)
 
         def quantise(name, raw, cast):
-            grouped = sb(name + "_bf", [P, P, PACK], BF16)
+            grouped = sb(name + "bf", [P, P, PACK], BF16)
             codes = sb(name + "_codes", [P, P], U32)
             scales = sb(name + "_scales", [P, P], U8)
             cast(grouped[:], raw.rearrange("p j w -> p w j"))
@@ -104,28 +104,31 @@ def tile_picked_wgatedg_none_l_kernel(tc, x_words, x_scales, w1, w2, w3, pos1, p
         nc.vector.tensor_copy(e_t[0][:, T // 2 : T], hi[:, 0 : T // 2])
 
         y_bank = {}
-        for step in PREP:
+        caster = {"A": nc.scalar.copy, "V": nc.vector.tensor_copy}
+
+        def prepare(step):
             b = int(step[1])
+            name = {"y": "w1", "e": "w2", "h": "w3"}[step[0]] + step[1]
+            raw = {"y": raw1[b][:], "e": raw2[b][:], "h": raw3[:, :, P * b : P * (b + 1)]}[step[0]]
+            wq = quantise(name, raw, caster[CAST.get(name, "A")])
             if step[0] == "y":
-                y_bank[b] = product(quantise("w1%d" % b, raw1[b][:], nc.scalar.copy), 0, T, step, "Y%d" % b)
-                if any(ADDER[3 * b + d] != "V" for d in range(3)):
-                    nc.scalar.copy(y_t[b][:], y_bank[b][:])
+                nc.scalar.copy(y_t[b][:], product(wq, 0, T, step, "Y%d" % b)[:])
             elif step[0] == "e":
-                nc.scalar.copy(e_t[1][:, 0:T], product(quantise("w21", raw2[1][:], nc.scalar.copy), 0, T, step, "A")[:])
+                nc.scalar.copy(e_t[b][:, 0:T], product(wq, 0, T, step, "A")[:])
             else:
-                wq = quantise("w3%d" % b, raw3[:, :, P * b : P * (b + 1)], nc.scalar.copy)
                 nc.scalar.copy(h_t[b][:, 0:T], product(wq, 0, T, step, "B")[:])
 
         engine = {"G": nc.gpsimd, "V": nc.vector}
         gates = {}
         terms = {}
         pairs = {}
+        sums = {}
         made = [[], []]
         turns = []
 
         def gate_of(u):
             b, d = divmod(u, 3)
-            picked = sb("eg%d" % u, [P, T], F32, AFTER.get("E%d" % u))
+            picked = sb("eg%d" % u, [P, T], F32)
             nc.vector.tensor_copy(picked[:], e_t[b][:].indirect(lists[d][:]))
             pre = sb("pre%d" % u, [P, T], F32)
             source = pre
@@ -151,7 +154,7 @@ def tile_picked_wgatedg_none_l_kernel(tc, x_words, x_scales, w1, w2, w3, pos1, p
 
         def term_of(u, pieces):
             b, d = divmod(u, 3)
-            picked = sb("hg%d" % u, [P, T], F32, AFTER.get("H%d" % u))
+            picked = sb("hg%d" % u, [P, T], F32)
             terms[u] = picked if MULER[u] == "C" else sb("term%d" % u, [P, T], F32)
             for c0, c1 in pieces:
                 looked_up = h_t[b][:].indirect(lists[d][:, c0 // 16 : c1 // 16])
@@ -161,6 +164,32 @@ def tile_picked_wgatedg_none_l_kernel(tc, x_words, x_scales, w1, w2, w3, pos1, p
                     nc.vector.tensor_copy(picked[:, c0:c1], looked_up)
                     engine[MULER[u]].tensor_tensor(terms[u][:, c0:c1], picked[:, c0:c1], gates[u][:, c0:c1], MULT)
             made[b].append(u)
+            if SUMMER[2 * b] == "P":
+                k = len(made[b])
+                count = 3 if SUMMER[2 * b + 1] == "P" else 2
+                if k == 1:
+                    sums[b] = psum.tile([P, T], F32, name="sum%d" % b, tag="Y%d" % b)
+                if k <= count:
+                    for j in range(4):
+                        cols = slice(P * j, P * (j + 1))
+                        nc.tensor.matmul(sums[b][:, cols], terms[u][:, cols], ident[:], start=(k == 1 and j == 0), stop=(k == count and j == 3), is_transpose=True)
+                if k == count:
+                    staged = sb("staged%d" % b, [P, T], F32)
+                    nc.scalar.copy(staged[:], sums[b][:])
+                    pairs[b] = psum.tile([P, T], F32, name="sumback%d" % b, tag="AB"[b])
+                    for j in range(4):
+                        cols = slice(P * j, P * (j + 1))
+                        nc.tensor.transpose(pairs[b][:, cols], staged[:, cols], ident[:])
+                if k == 3:
+                    total = sb("total%d" % b, [P, T], F32)
+                    if count == 3:
+                        nc.scalar.copy(total[:], pairs[b][:])
+                        nc.sync.dma_start(out[P * b : P * (b + 1), :], total[:])
+                    else:
+                        for c0, c1 in pieces:
+                            nc.vector.tensor_tensor(total[:, c0:c1], terms[u][:, c0:c1], pairs[b][:, c0:c1], ADD)
+                            nc.sync.dma_start(out[P * b : P * (b + 1), c0:c1], total[:, c0:c1])
+                return
             if len(made[b]) == 2:
                 pairs[b] = sb("pair%d" % b, [P, T], F32)
                 engine[SUMMER[2 * b]].tensor_tensor(pairs[b][:], terms[made[b][0]][:], terms[made[b][1]][:], ADD)
@@ -171,7 +200,9 @@ def tile_picked_wgatedg_none_l_kernel(tc, x_words, x_scales, w1, w2, w3, pos1, p
                     nc.sync.dma_start(out[P * b : P * (b + 1), c0:c1], total[:, c0:c1])
 
         for step in ORDER:
-            if step[0] == "E":
+            if step[0] in "yeh":
+                prepare(step)
+            elif step[0] == "E":
                 gate_of(int(step[1]))
             else:
                 term_of(int(step[1]), [(0, T // 2), (T // 2, T)] if step == ORDER[-1] else [(0, T)])

@@ -22,12 +22,12 @@ P = 128
 PACK = 4
 WINDOW = 704
 
-AFTER = {"pre4": "w31bf", "pre3": "eg4", "gate3": "w10bf", "eg1": "eg5", "pre1": "w31bf", "gate1": "eg0", "pre2": "w20bf", "gate2": "eg5", "hg4": "e1", "hg2": "gate4", "hg3": "pre5", "hg0": "w21bf"}
-ADDER = ["G", "P", "G", "G", "P", "P"]
+AFTER = {"w10bf": "w20bf", "hg4": "pre5", "w30bf": "w20bf", "eg1": "eg4", "pre1": "hg3", "pre2": "w21bf", "gate2": "pre5", "hg5": "pre3", "hg1": "eg3"}
+ADDER = ["P", "P", "G", "G", "G", "V"]
 MULER = ["C", "C", "C", "C", "C", "C"]
 SUMMER = ["V", "V", "P", "P"]
-CAST = {}
-ORDER = ["y0", "e1", "y1", "E5", "h1", "E4", "E0", "H5", "E3", "E1", "E2", "H4", "h0", "H2", "H3", "H0", "H1"]
+CAST = {"w30": "A", "w10": "A", "w21": "A", "w11": "A", "w31": "A"}
+ORDER = ["y1", "e1", "E5", "y0", "E4", "h1", "E3", "E0", "H4", "h0", "H0", "H3", "E1", "E2", "H5", "H2", "H1"]
 
 
 def tile_picked_wgatedg_none_l_kernel(tc, x_words, x_scales, w1, w2, w3, pos1, pos2, pos3, out):
@@ -68,8 +68,8 @@ def tile_picked_wgatedg_none_l_kernel(tc, x_words, x_scales, w1, w2, w3, pos1, p
         for q in range(4):
             nc.sync.dma_start(xs[32 * q : 32 * q + 4, :].bitcast(I32), x_scales[0, 4 * q : 4 * q + 4, :].bitcast(I32))
         nc.sync.dma_start(raw2[1][:], rows(w2)[:, :, P:N])
-        nc.sync.dma_start(raw1[1][:], rows(w1)[:, :, P:N])
         nc.sync.dma_start(raw1[0][:], rows(w1)[:, :, 0:P])
+        nc.sync.dma_start(raw1[1][:], rows(w1)[:, :, P:N])
         nc.sync.dma_start(lists[2][:], pos3)
         nc.sync.dma_start(lists[1][:], pos2)
         nc.sync.dma_start(raw3[:], rows(w3))
@@ -112,7 +112,8 @@ def tile_picked_wgatedg_none_l_kernel(tc, x_words, x_scales, w1, w2, w3, pos1, p
             raw = {"y": raw1[b][:], "e": raw2[b][:], "h": raw3[:, :, P * b : P * (b + 1)]}[step[0]]
             wq = quantise(name, raw, caster[CAST.get(name, "A")])
             if step[0] == "y":
-                nc.scalar.copy(y_t[b][:], product(wq, 0, T, step, "Y%d" % b)[:])
+                y_bank[b] = product(wq, 0, T, step, "Y%d" % b)
+                nc.scalar.copy(y_t[b][:], y_bank[b][:])
             elif step[0] == "e":
                 nc.scalar.copy(e_t[b][:, 0:T], product(wq, 0, T, step, "A")[:])
             else:

from contextlib import ExitStack

import concourse.mybir as mybir
from concourse.masks import make_identity

K, T, N = 512, 512, 256
FLOPS = 3 * 2 * K * T * N

F32 = mybir.dt.float32
BF16 = mybir.dt.bfloat16
I32 = mybir.dt.int32
U32 = mybir.dt.uint32
U16 = mybir.dt.uint16
U8 = mybir.dt.uint8
FP8X4 = mybir.dt.float8_e4m3fn_x4
FP4X4 = mybir.dt.float4_e2m1fn_x4
MULT = mybir.AluOpType.mult
ADD = mybir.AluOpType.add
SIGMOID = mybir.ActivationFunctionType.Sigmoid

P = 128
PACK = 4
WINDOW = 704

AFTER = {"w10bf": "w20bf", "hg4": "pre5", "w30bf": "w20bf", "eg1": "eg4", "pre1": "hg3", "pre2": "w21bf", "gate2": "pre5", "hg5": "pre3", "hg1": "eg3"}
ADDER = ["P", "P", "G", "G", "G", "V"]
MULER = ["C", "C", "C", "C", "C", "C"]
SUMMER = ["V", "V", "P", "P"]
CAST = {"w30": "A", "w10": "A", "w21": "A", "w11": "A", "w31": "A"}
ORDER = ["y1", "e1", "E5", "y0", "E4", "h1", "E3", "E0", "H4", "h0", "H0", "H3", "E1", "E2", "H5", "H2", "H1"]


def tile_picked_wgatedg_none_l_kernel(tc, x_words, x_scales, w1, w2, w3, pos1, pos2, pos3, out):
    nc = tc.nc
    with ExitStack() as ctx:
        keep = ctx.enter_context(tc.tile_pool(name="keep", bufs=1))
        psum = ctx.enter_context(tc.psum_pool(name="psum", bufs=1))

        def sb(name, shape, dtype):
            return keep.tile(shape, dtype, name=name, tag=AFTER.get(name, name), align_bytes=64)

        xw = sb("xw", [P, 2 * T], U8)
        xs = sb("xs", [P, T], U8)
        lists = [sb("pos%d" % d, [P, T // 16], U16) for d in range(3)]
        raw2 = [sb("raw2_%d" % b, [P, PACK, P], F32) for b in range(2)]
        raw1 = [sb("raw1_%d" % b, [P, PACK, P], F32) for b in range(2)]
        raw3 = sb("raw3", [P, PACK, N], F32)
        e_t = [sb("e%d" % b, [P, WINDOW], F32) for b in range(2)]
        h_t = [sb("h%d" % b, [P, WINDOW], F32) for b in range(2)]
        y_t = [sb("y%d" % b, [P, T], F32) for b in range(2)]
        warm = sb("warm", [P, 2], F32)
        ident = sb("ident", [P, P], F32)

        nc.vector.memset(xs[:].bitcast(I32), 0)
        nc.vector.memset(warm[:, 0:1], 0.0)
        nc.scalar.activation(warm[:, 1:2], warm[:, 0:1], SIGMOID)
        make_identity(nc, ident[:])
        for b in range(2):
            nc.gpsimd.memset(e_t[b][:, T:WINDOW], 0.0)
        for b in range(2):
            nc.gpsimd.memset(h_t[b][:, T:WINDOW], 0.0)

        def rows(w):
            return w.rearrange("(p j) n -> p j n", j=PACK)

        nc.sync.dma_start(raw2[0][:], rows(w2)[:, :, 0:P])
        nc.sync.dma_start(xw[:].bitcast(I32), x_words[0].bitcast(I32))
        for q in range(4):
            nc.sync.dma_start(xs[32 * q : 32 * q + 4, :].bitcast(I32), x_scales[0, 4 * q : 4 * q + 4, :].bitcast(I32))
        nc.sync.dma_start(raw2[1][:], rows(w2)[:, :, P:N])
        nc.sync.dma_start(raw1[0][:], rows(w1)[:, :, 0:P])
        nc.sync.dma_start(raw1[1][:], rows(w1)[:, :, P:N])
        nc.sync.dma_start(lists[2][:], pos3)
        nc.sync.dma_start(lists[1][:], pos2)
        nc.sync.dma_start(raw3[:], rows(w3))
        nc.sync.dma_start(lists[0][:], pos1)

        def quantise(name, raw, cast):
            grouped = sb(name + "bf", [P, P, PACK], BF16)
            codes = sb(name + "_codes", [P, P], U32)
            scales = sb(name + "_scales", [P, P], U8)
            cast(grouped[:], raw.rearrange("p j w -> p w j"))
            nc.vector.quantize_mx(codes[:].bitcast(FP8X4), scales[:], grouped[:].rearrange("p w j -> p (w j)"))
            return codes, scales

        def product(wq, c0, c1, name, tag):
            bank = psum.tile([P, T], F32, name=name, tag=tag)
            codes, scales = wq
            nc.tensor.matmul_mx(
                bank[:, 0 : c1 - c0],
                lhsT=codes[:].bitcast(FP8X4),
                lhsT_scale=scales[:],
                rhs=xw[:, 2 * c0 : 2 * c1].bitcast(FP4X4),
                rhs_scale=xs[:, c0:c1],
                start=True,
                stop=True,
            )
            return bank

        q20 = quantise("w20", raw2[0][:], nc.vector.tensor_copy)
        lo = product(q20, 0, T // 2, "e0a", "A")
        hi = product(q20, T // 2, T, "e0b", "B")
        nc.vector.tensor_copy(e_t[0][:, 0 : T // 2], lo[:, 0 : T // 2])
        nc.vector.tensor_copy(e_t[0][:, T // 2 : T], hi[:, 0 : T // 2])

        y_bank = {}
        caster = {"A": nc.scalar.copy, "V": nc.vector.tensor_copy}

        def prepare(step):
            b = int(step[1])
            name = {"y": "w1", "e": "w2", "h": "w3"}[step[0]] + step[1]
            raw = {"y": raw1[b][:], "e": raw2[b][:], "h": raw3[:, :, P * b : P * (b + 1)]}[step[0]]
            wq = quantise(name, raw, caster[CAST.get(name, "A")])
            if step[0] == "y":
                y_bank[b] = product(wq, 0, T, step, "Y%d" % b)
                nc.scalar.copy(y_t[b][:], y_bank[b][:])
            elif step[0] == "e":
                nc.scalar.copy(e_t[b][:, 0:T], product(wq, 0, T, step, "A")[:])
            else:
                nc.scalar.copy(h_t[b][:, 0:T], product(wq, 0, T, step, "B")[:])

        engine = {"G": nc.gpsimd, "V": nc.vector}
        gates = {}
        terms = {}
        pairs = {}
        sums = {}
        made = [[], []]
        turns = []

        def gate_of(u):
            b, d = divmod(u, 3)
            picked = sb("eg%d" % u, [P, T], F32)
            nc.vector.tensor_copy(picked[:], e_t[b][:].indirect(lists[d][:]))
            pre = sb("pre%d" % u, [P, T], F32)
            source = pre
            if ADDER[u] == "G":
                nc.gpsimd.tensor_tensor(pre[:], picked[:], y_t[b][:], ADD)
            elif ADDER[u] == "V":
                nc.vector.tensor_tensor(pre[:], picked[:], y_bank[b][:], ADD)
            else:
                k = len(turns) % 2
                turns.append(u)
                turned = psum.tile([P, T], F32, name="turned%d" % u, tag="turn%d" % k)
                for i, src in enumerate((y_t[b], picked)):
                    for j in range(4):
                        cols = slice(P * j, P * (j + 1))
                        nc.tensor.matmul(turned[:, cols], src[:, cols], ident[:], start=(i == 0 and j == 0), stop=(i == 1 and j == 3), is_transpose=True)
                nc.scalar.copy(pre[:], turned[:])
                source = psum.tile([P, T], F32, name="back%d" % u, tag="back%d" % k)
                for j in range(4):
                    cols = slice(P * j, P * (j + 1))
                    nc.tensor.transpose(source[:, cols], pre[:, cols], ident[:])
            gates[u] = sb("gate%d" % u, [P, T], F32)
            nc.scalar.activation(gates[u][:], source[:], SIGMOID)

        def term_of(u, pieces):
            b, d = divmod(u, 3)
            picked = sb("hg%d" % u, [P, T], F32)
            terms[u] = picked if MULER[u] == "C" else sb("term%d" % u, [P, T], F32)
            for c0, c1 in pieces:
                looked_up = h_t[b][:].indirect(lists[d][:, c0 // 16 : c1 // 16])
                if MULER[u] == "C":
                    nc.vector.tensor_tensor(picked[:, c0:c1], looked_up, gates[u][:, c0:c1], MULT)
                else:
                    nc.vector.tensor_copy(picked[:, c0:c1], looked_up)
                    engine[MULER[u]].tensor_tensor(terms[u][:, c0:c1], picked[:, c0:c1], gates[u][:, c0:c1], MULT)
            made[b].append(u)
            if SUMMER[2 * b] == "P":
                k = len(made[b])
                count = 3 if SUMMER[2 * b + 1] == "P" else 2
                if k == 1:
                    sums[b] = psum.tile([P, T], F32, name="sum%d" % b, tag="Y%d" % b)
                if k <= count:
                    for j in range(4):
                        cols = slice(P * j, P * (j + 1))
                        nc.tensor.matmul(sums[b][:, cols], terms[u][:, cols], ident[:], start=(k == 1 and j == 0), stop=(k == count and j == 3), is_transpose=True)
                if k == count:
                    staged = sb("staged%d" % b, [P, T], F32)
                    nc.scalar.copy(staged[:], sums[b][:])
                    pairs[b] = psum.tile([P, T], F32, name="sumback%d" % b, tag="AB"[b])
                    for j in range(4):
                        cols = slice(P * j, P * (j + 1))
                        nc.tensor.transpose(pairs[b][:, cols], staged[:, cols], ident[:])
                if k == 3:
                    total = sb("total%d" % b, [P, T], F32)
                    if count == 3:
                        nc.scalar.copy(total[:], pairs[b][:])
                        nc.sync.dma_start(out[P * b : P * (b + 1), :], total[:])
                    else:
                        for c0, c1 in pieces:
                            nc.vector.tensor_tensor(total[:, c0:c1], terms[u][:, c0:c1], pairs[b][:, c0:c1], ADD)
                            nc.sync.dma_start(out[P * b : P * (b + 1), c0:c1], total[:, c0:c1])
                return
            if len(made[b]) == 2:
                pairs[b] = sb("pair%d" % b, [P, T], F32)
                engine[SUMMER[2 * b]].tensor_tensor(pairs[b][:], terms[made[b][0]][:], terms[made[b][1]][:], ADD)
            if len(made[b]) == 3:
                total = sb("total%d" % b, [P, T], F32)
                for c0, c1 in pieces:
                    engine[SUMMER[2 * b + 1]].tensor_tensor(total[:, c0:c1], pairs[b][:, c0:c1], terms[u][:, c0:c1], ADD)
                    nc.sync.dma_start(out[P * b : P * (b + 1), c0:c1], total[:, c0:c1])

        for step in ORDER:
            if step[0] in "yeh":
                prepare(step)
            elif step[0] == "E":
                gate_of(int(step[1]))
            else:
                term_of(int(step[1]), [(0, T // 2), (T // 2, T)] if step == ORDER[-1] else [(0, T)])
